import numpy as np
import ml_dtypes


def mxq(x, axis, fmt="e4m3"):
    dtype, down = {"e4m3": (ml_dtypes.float8_e4m3fn, 7), "e5m2": (ml_dtypes.float8_e5m2, 14)}[fmt]
    v = np.moveaxis(np.asarray(x, np.float32).astype(ml_dtypes.bfloat16).astype(np.float64), axis, -1)
    blocks = v.reshape(v.shape[:-1] + (-1, 32))
    amax = np.abs(blocks).max(-1, keepdims=True)
    byte = np.maximum(np.where(amax > 0, np.frexp(amax)[1] - 1 + 127, 0) - down, 1)
    scale = np.exp2(byte - 127.0)
    codes = (blocks / scale).astype(np.float32).astype(dtype).astype(np.float64)
    return np.moveaxis((codes * scale).reshape(v.shape), -1, axis)


WIDE = False


def mx_kscale(k):
    if not WIDE:
        return np.ones(k)
    levels = np.array([10, -10, 5, -5, 0])
    if k % 512:
        return np.exp2(np.random.permutation(np.resize(levels, k // 32))).repeat(32)
    a = np.empty((k // 512, 16))
    for p in range(k // 512):
        a[p, :8] = np.random.permutation(np.resize(levels, 8))
        for g in range(8):
            far = levels[np.abs(levels - a[p, g]) >= 10]
            a[p, g + 8] = far[np.random.randint(len(far))]
    return np.exp2(a.ravel()).repeat(32)


def f64(x):
    return np.asarray(x).astype(np.float64)


def striped8(idx):
    return np.concatenate([x.reshape(-1, 16).T for x in idx]).astype(np.uint16)


def runs(offs, k):
    lists = np.stack([offs[16 * r : 16 * r + 16].T.reshape(-1) for r in range(8)]).astype(np.int64)
    return lists[np.arange(k) % 512 // 64]


def pack_weight(w):
    k, n = w.shape
    w = f64(np.asarray(w, np.float32).astype(ml_dtypes.bfloat16)).reshape(k // 32, 32, n)
    amax = np.abs(w).max(1)
    byte = np.clip(np.where(amax > 0, np.frexp(amax)[1] - 1 + 127 - 7, 1), 1, 254)
    scaled = (w * np.exp2(127.0 - byte)[:, None, :]).reshape(k, n).astype(np.float32)
    words = np.ascontiguousarray(scaled.reshape(k // 512, 128, 4, n).transpose(0, 1, 3, 2)).astype(ml_dtypes.float8_e4m3fn).view(np.uint8)
    return words, np.ascontiguousarray(byte.astype(np.uint8).reshape(k // 512, 16, n))


def unpack_weight(words, scales):
    g, p, n, _ = words.shape
    vals = np.ascontiguousarray(words).view(ml_dtypes.float8_e4m3fn).astype(np.float64) * np.repeat(np.exp2(scales.astype(np.float64) - 127.0), 8, axis=1)[..., None]
    return vals.transpose(0, 1, 3, 2).reshape(g * 512, n)


K, T, S, V, N, H = 512, 2048, 512, 256, 512, 512


def setup_inputs():
    n = np.random.standard_normal
    s = mx_kscale(K)[:, None]
    u = mx_kscale(H)
    packed_xT = pack_weight(n((K, T)) * s)
    perm = np.stack([np.random.permutation(S) for _ in range(8)])
    return {
        "x_words": packed_xT[0],
        "x_scales": packed_xT[1],
        "w1": (n((K, H)) / np.sqrt(K) / s * u).astype(np.float32),
        "w2": (n((H, N)) / np.sqrt(H) / u[:, None]).astype(np.float32),
        "offs": striped8(np.stack([np.random.permutation(T)[:S] for _ in range(8)])),
        "la": striped8(perm[:, :V]),
        "lb": striped8(perm[:, V:]),
    }


def reference(x_words, x_scales, w1, w2, offs, la, lb):
    xq = unpack_weight(x_words, x_scales)[np.arange(K)[:, None], runs(offs, K)]
    y = mxq(f64(w1), 0, "e4m3").T @ xq
    a = y[np.arange(H)[:, None], runs(la, H)]
    b = y[np.arange(H)[:, None], runs(lb, H)]
    mx = np.maximum(a, b)
    mn = np.minimum(a, b)
    p = np.zeros((H, S))
    p[np.arange(H)[:, None], runs(la, H)] = mn
    zs = p.copy()
    zs[np.arange(H)[:, None], runs(lb, H)] = mx
    return mxq(f64(w2), 0, "e4m3").T @ mxq(zs, 0, "e4m3")

@@ -1,0 +1,159 @@
+from contextlib import ExitStack
+
+import concourse.mybir as mybir
+
+K, T, S, V, H, N = 512, 2048, 512, 256, 512, 512
+FLOPS = 2 * K * H * S + 2 * H * N * S
+
+F32 = mybir.dt.float32
+BF16 = mybir.dt.bfloat16
+I32 = mybir.dt.int32
+U32 = mybir.dt.uint32
+U16 = mybir.dt.uint16
+U8 = mybir.dt.uint8
+FP8X4 = mybir.dt.float8_e4m3fn_x4
+ALU = mybir.AluOpType
+
+P = 128
+PACK = 4
+HALF = S // 2
+PLANE_ORDER = (2, 0, 1, 3)
+W1_SPLIT = 88
+TAIL_SPLIT = 176
+
+
+def tile_picked_sortpair_none_p_kernel(tc, x_words, x_scales, w1, w2, offs, la, lb, out):
+    nc = tc.nc
+    with ExitStack() as ctx:
+        keep = ctx.enter_context(tc.tile_pool(name="keep", bufs=1))
+        ring = ctx.enter_context(tc.tile_pool(name="ring", bufs=3))
+        psum = ctx.enter_context(tc.psum_pool(name="psum", bufs=1))
+
+        offs_t = keep.tile([P, S // 16], U16, name="offs_t")
+        la_t = keep.tile([P, V // 16], U16, name="la_t")
+        lb_t = keep.tile([P, V // 16], U16, name="lb_t")
+        words_all = keep.tile([P, T], U32, name="words_all", align_bytes=64)
+        scales_all = keep.tile([P, T], U8, name="scales_all", align_bytes=64)
+        scales_picked = keep.tile([P, S], U8, name="scales_picked", align_bytes=64)
+        x_scale = keep.tile([P, S], U8, name="x_scale", align_bytes=64)
+        x_code = [keep.tile([P, HALF], U32, name="x_code%d" % h, align_bytes=64) for h in range(2)]
+        w1_raw = keep.tile([P, PACK, H], F32, name="w1_raw", tag="w_raw", align_bytes=64)
+        w1_bf = keep.tile([P, PACK * H], BF16, name="w1_bf", align_bytes=64)
+        w2_bf = keep.tile([P, PACK * N], BF16, name="w2_bf", align_bytes=64)
+        w1_code = keep.tile([P, H], U32, name="w1_code", align_bytes=64)
+        w1_scale = keep.tile([P, H], U8, name="w1_scale", align_bytes=64)
+        w2_code = keep.tile([P, N], U32, name="w2_code", align_bytes=64)
+        w2_scale = keep.tile([P, N], U8, name="w2_scale", align_bytes=64)
+        z_bf = keep.tile([P, S, PACK], BF16, name="z_bf", align_bytes=64)
+        z_code = keep.tile([P, S], U32, name="z_code", align_bytes=64)
+        z_scale = keep.tile([P, S], U8, name="z_scale", align_bytes=64)
+
+        nc.vector.memset(scales_all[:].bitcast(I32), 0)
+        nc.gpsimd.memset(x_scale[:].bitcast(I32), 0)
+
+        nc.sync.dma_start(offs_t[:], offs)
+        nc.sync.dma_start(scales_all[0:P:8, :].bitcast(I32), x_scales[0].bitcast(I32))
+        nc.sync.dma_start(w1_raw[:], w1.rearrange("(p j) c -> p j c", j=PACK))
+        nc.sync.dma_start(words_all[:].bitcast(I32), x_words[0].rearrange("p n t -> p (n t)").bitcast(I32))
+        nc.sync.dma_start(la_t[:], la)
+        nc.sync.dma_start(lb_t[:], lb)
+
+        nc.vector.tensor_copy(scales_picked[:], scales_all[:].indirect(offs_t[:]))
+        for c in range(4):
+            nc.scalar.dma_start(x_scale[c:P:32, :].bitcast(I32), scales_picked[8 * c : P : 32, :].bitcast(I32))
+
+        w1_dst = w1_bf[:].rearrange("p (t m j) -> p m t j", t=PACK, j=PACK)
+        w1_src = w1_raw[:].rearrange("p j (m t) -> p m t j", t=PACK)
+        nc.vector.tensor_copy(w1_dst[:, :W1_SPLIT], w1_src[:, :W1_SPLIT])
+        nc.scalar.copy(w1_dst[:, W1_SPLIT:], w1_src[:, W1_SPLIT:])
+
+        w2_raw = keep.tile([P, PACK, N], F32, name="w2_raw", tag="w_raw", align_bytes=64)
+        nc.sync.dma_start(w2_raw[:], w2.rearrange("(p j) c -> p j c", j=PACK))
+
+        def quantize(code, scale, src, lo, hi):
+            nc.vector.quantize_mx(
+                out=code[:, lo:hi].bitcast(FP8X4), scales=scale[:, lo:hi], in_=src[:, PACK * lo : PACK * hi]
+            )
+
+        def product(acc, w_code, w_scale, block, rhs, rhs_scale):
+            cols = slice(block * P, (block + 1) * P)
+            nc.tensor.matmul_mx(
+                out=acc,
+                lhsT=w_code[:, cols].bitcast(FP8X4),
+                lhsT_scale=w_scale[:, cols],
+                rhs=rhs.bitcast(FP8X4),
+                rhs_scale=rhs_scale,
+                start=True,
+                stop=True,
+            )
+
+        def half(h):
+            return slice(h * HALF, (h + 1) * HALF)
+
+        quantize(w1_code, w1_scale, w1_bf, 2 * P, 4 * P)
+        for h in range(2):
+            nc.vector.tensor_copy(x_code[h][:], words_all[:].indirect(offs_t[:, 16 * h : 16 * (h + 1)]))
+        quantize(w1_code, w1_scale, w1_bf, 0, 2 * P)
+
+        y = []
+        for s, t in enumerate(PLANE_ORDER):
+            y_s = keep.tile([P, S], F32, name="y%d" % s)
+            for h in range(2):
+                acc = psum.tile([P, HALF], F32, name="acc", tag="bank%d" % (2 * s + h))
+                product(acc[:], w1_code, w1_scale, t, x_code[h][:], x_scale[:, half(h)])
+                nc.scalar.copy(y_s[:, half(h)], acc[:])
+            y.append(y_s)
+
+        for h in range(2):
+            cols = slice(h * N // 2, (h + 1) * N // 2)
+            nc.scalar.copy(
+                w2_bf[:].rearrange("p (n j) -> p n j", j=PACK)[:, cols].rearrange("p (c i) j -> p c j i", i=4),
+                w2_raw[:, :, cols].rearrange("p j (c i) -> p c j i", i=4),
+            )
+
+        a = [keep.tile([P, V], F32, name="a%d" % s) for s in range(PACK)]
+        b = [keep.tile([P, V], F32, name="b%d" % s) for s in range(PACK)]
+        low = [keep.tile([P, V], F32, name="low%d" % s) for s in range(PACK)]
+        high = [keep.tile([P, V], F32, name="high%d" % s) for s in range(PACK)]
+
+        def fetch(dst, s, lst):
+            nc.vector.tensor_copy(dst[s][:], y[s][:].indirect(lst[:]))
+
+        fetch(a, 0, la_t)
+        fetch(b, 0, lb_t)
+        fetch(a, 1, la_t)
+        for s, t in enumerate(PLANE_ORDER):
+            nc.vector.tensor_tensor(low[s][:], a[s][:], b[s][:], ALU.min)
+            nc.vector.tensor_tensor(high[s][:], a[s][:], b[s][:], ALU.max)
+            if s + 1 < PACK:
+                fetch(b, s + 1, lb_t)
+            z = ring.tile([P, S], F32, name="z")
+            nc.vector.tensor_copy(z[:].indirect(la_t[:]), low[s][:])
+            if s + 2 < PACK:
+                fetch(a, s + 2, la_t)
+            else:
+                h = s + 2 - PACK
+                quantize(w2_code, w2_scale, w2_bf, h * N // 2, (h + 1) * N // 2)
+            nc.vector.tensor_copy(z[:].indirect(lb_t[:]), high[s][:])
+            if s + 1 < PACK:
+                nc.scalar.copy(z_bf[:, :, t], z[:])
+            else:
+                for h in range(2):
+                    lo, mid, hi = h * HALF, h * HALF + TAIL_SPLIT, (h + 1) * HALF
+                    nc.vector.tensor_copy(z_bf[:, lo:mid, t], z[:, lo:mid])
+                    nc.scalar.copy(z_bf[:, mid:hi, t], z[:, mid:hi])
+
+        z_flat = z_bf[:].rearrange("p j t -> p (j t)")
+        for h in range(2):
+            quantize(z_code, z_scale, z_flat, h * HALF, (h + 1) * HALF)
+
+        for m in range(N // P):
+            res = keep.tile([P, S], F32, name="res%d" % m)
+            for h in range(2):
+                acc = psum.tile([P, HALF], F32, name="acc", tag="bank%d" % (2 * m + h))
+                product(acc[:], w2_code, w2_scale, m, z_code[:, half(h)], z_scale[:, half(h)])
+                if h == 0:
+                    nc.scalar.copy(res[:, half(h)], acc[:])
+                else:
+                    nc.vector.tensor_copy(res[:, half(h)], acc[:])
+            nc.sync.dma_start(out[m * P : (m + 1) * P, :], res[:])

@@ -17,9 +17,8 @@ ALU = mybir.AluOpType
 P = 128
 PACK = 4
 HALF = S // 2
-PLANE_ORDER = (2, 0, 1, 3)
-W1_SPLIT = 88
-TAIL_SPLIT = 176
+PLANE_ORDER = (0, 2, 3, 1)
+CHUNKS = ((0, 128), (128, 256), (256, 512))
 
 
 def tile_picked_sortpair_none_p_kernel(tc, x_words, x_scales, w1, w2, offs, la, lb, out):
@@ -29,6 +28,12 @@ def tile_picked_sortpair_none_p_kernel(tc, x_words, x_scales, w1, w2, offs, la, 
         ring = ctx.enter_context(tc.tile_pool(name="ring", bufs=3))
         psum = ctx.enter_context(tc.psum_pool(name="psum", bufs=1))
 
+        def tiles(name, count, shape, dtype):
+            return [keep.tile(shape, dtype, name="%s%d" % (name, i), align_bytes=64) for i in range(count)]
+
+        def half(h):
+            return slice(h * HALF, (h + 1) * HALF)
+
         offs_t = keep.tile([P, S // 16], U16, name="offs_t")
         la_t = keep.tile([P, V // 16], U16, name="la_t")
         lb_t = keep.tile([P, V // 16], U16, name="lb_t")
@@ -36,44 +41,43 @@ def tile_picked_sortpair_none_p_kernel(tc, x_words, x_scales, w1, w2, offs, la, 
         scales_all = keep.tile([P, T], U8, name="scales_all", align_bytes=64)
         scales_picked = keep.tile([P, S], U8, name="scales_picked", align_bytes=64)
         x_scale = keep.tile([P, S], U8, name="x_scale", align_bytes=64)
-        x_code = [keep.tile([P, HALF], U32, name="x_code%d" % h, align_bytes=64) for h in range(2)]
-        w1_raw = keep.tile([P, PACK, H], F32, name="w1_raw", tag="w_raw", align_bytes=64)
-        w1_bf = keep.tile([P, PACK * H], BF16, name="w1_bf", align_bytes=64)
-        w2_bf = keep.tile([P, PACK * N], BF16, name="w2_bf", align_bytes=64)
-        w1_code = keep.tile([P, H], U32, name="w1_code", align_bytes=64)
-        w1_scale = keep.tile([P, H], U8, name="w1_scale", align_bytes=64)
-        w2_code = keep.tile([P, N], U32, name="w2_code", align_bytes=64)
-        w2_scale = keep.tile([P, N], U8, name="w2_scale", align_bytes=64)
-        z_bf = keep.tile([P, S, PACK], BF16, name="z_bf", align_bytes=64)
-        z_code = keep.tile([P, S], U32, name="z_code", align_bytes=64)
-        z_scale = keep.tile([P, S], U8, name="z_scale", align_bytes=64)
+        x_code = keep.tile([P, S], U32, name="x_code", align_bytes=64)
+        w1_head = keep.tile([P, 2, H], F32, name="w1_head", align_bytes=64)
+        w1_last = keep.tile([P, 2, H], F32, name="w1_last", align_bytes=64)
+        w1_bf = [
+            keep.tile([P, 2, P, PACK], BF16, name="w1_bf0", align_bytes=64),
+            keep.tile([P, 2, P, PACK], BF16, name="w1_bf1", tag="late", align_bytes=64),
+        ]
+        w1_code = tiles("w1_code", PACK, [P, P], U32)
+        w1_scale = tiles("w1_scale", PACK, [P, P], U8)
+        w2_bf = tiles("w2_bf", 2, [P, HALF, PACK], BF16)
+        w2_code = tiles("w2_code", 2, [P, HALF], U32)
+        w2_scale = tiles("w2_scale", 2, [P, HALF], U8)
+        z_bf = [keep.tile([P, hi - lo, PACK], BF16, name="z_bf%d" % lo, align_bytes=64) for lo, hi in CHUNKS]
+        z_code = [keep.tile([P, hi - lo], U32, name="z_code%d" % lo, align_bytes=64) for lo, hi in CHUNKS]
+        z_scale = [keep.tile([P, hi - lo], U8, name="z_scale%d" % lo, align_bytes=64) for lo, hi in CHUNKS]
 
         nc.vector.memset(scales_all[:].bitcast(I32), 0)
-        nc.gpsimd.memset(x_scale[:].bitcast(I32), 0)
+        nc.vector.memset(x_scale[:].bitcast(I32), 0)
 
+        w1_rows = w1.rearrange("(p j) c -> p j c", j=PACK)
+        words_hbm = x_words[0].rearrange("p n t -> p (n t)").bitcast(I32)
         nc.sync.dma_start(offs_t[:], offs)
+        nc.sync.dma_start(words_all[:, : T // 2].bitcast(I32), words_hbm[:, : T // 2])
         nc.sync.dma_start(scales_all[0:P:8, :].bitcast(I32), x_scales[0].bitcast(I32))
-        nc.sync.dma_start(w1_raw[:], w1.rearrange("(p j) c -> p j c", j=PACK))
-        nc.sync.dma_start(words_all[:].bitcast(I32), x_words[0].rearrange("p n t -> p (n t)").bitcast(I32))
+        nc.sync.dma_start(words_all[:, T // 2 :].bitcast(I32), words_hbm[:, T // 2 :])
+        nc.sync.dma_start(w1_head[:], w1_rows[:, :2])
+        nc.sync.dma_start(w1_last[:], w1_rows[:, 2:])
         nc.sync.dma_start(la_t[:], la)
         nc.sync.dma_start(lb_t[:], lb)
 
         nc.vector.tensor_copy(scales_picked[:], scales_all[:].indirect(offs_t[:]))
         for c in range(4):
             nc.scalar.dma_start(x_scale[c:P:32, :].bitcast(I32), scales_picked[8 * c : P : 32, :].bitcast(I32))
+        nc.vector.tensor_copy(x_code[:], words_all[:].indirect(offs_t[:]))
 
-        w1_dst = w1_bf[:].rearrange("p (t m j) -> p m t j", t=PACK, j=PACK)
-        w1_src = w1_raw[:].rearrange("p j (m t) -> p m t j", t=PACK)
-        nc.vector.tensor_copy(w1_dst[:, :W1_SPLIT], w1_src[:, :W1_SPLIT])
-        nc.scalar.copy(w1_dst[:, W1_SPLIT:], w1_src[:, W1_SPLIT:])
-
-        w2_raw = keep.tile([P, PACK, N], F32, name="w2_raw", tag="w_raw", align_bytes=64)
-        nc.sync.dma_start(w2_raw[:], w2.rearrange("(p j) c -> p j c", j=PACK))
-
-        def quantize(code, scale, src, lo, hi):
-            nc.vector.quantize_mx(
-                out=code[:, lo:hi].bitcast(FP8X4), scales=scale[:, lo:hi], in_=src[:, PACK * lo : PACK * hi]
-            )
+        def quantize(code, scale, src):
+            nc.vector.quantize_mx(out=code[:].bitcast(FP8X4), scales=scale[:], in_=src)
 
         def product(acc, w_code, w_scale, block, rhs, rhs_scale):
             cols = slice(block * P, (block + 1) * P)
@@ -87,28 +91,32 @@ def tile_picked_sortpair_none_p_kernel(tc, x_words, x_scales, w1, w2, offs, la, 
                 stop=True,
             )
 
-        def half(h):
-            return slice(h * HALF, (h + 1) * HALF)
-
-        quantize(w1_code, w1_scale, w1_bf, 2 * P, 4 * P)
-        for h in range(2):
-            nc.vector.tensor_copy(x_code[h][:], words_all[:].indirect(offs_t[:, 16 * h : 16 * (h + 1)]))
-        quantize(w1_code, w1_scale, w1_bf, 0, 2 * P)
+        head_src = w1_head[:].rearrange("p j (m u v) -> p v m u j", u=2, v=2)
+        last_src = w1_last[:].rearrange("p j (m u v) -> p v m u j", u=2, v=2)
+        copies = (nc.vector.tensor_copy, nc.scalar.copy)
+        for v in range(2):
+            copies[v](w1_bf[v][:, :, :, :2].rearrange("p u m j -> p m u j"), head_src[:, v])
+        for u in range(2):
+            nc.vector.tensor_copy(w1_bf[0][:, u, :, 2:], last_src[:, 0, :, u])
+        nc.scalar.copy(w1_bf[1][:, :, :, 2:].rearrange("p u m j -> p m u j"), last_src[:, 1])
+        for t in PLANE_ORDER:
+            quantize(w1_code[t], w1_scale[t], w1_bf[t % 2][:, t // 2].rearrange("p m j -> p (m j)"))
+        w2_raw = keep.tile([P, PACK, N], F32, name="w2_raw", tag="late", align_bytes=64)
+        nc.sync.dma_start(w2_raw[:], w2.rearrange("(p j) c -> p j c", j=PACK))
 
         y = []
         for s, t in enumerate(PLANE_ORDER):
             y_s = keep.tile([P, S], F32, name="y%d" % s)
             for h in range(2):
                 acc = psum.tile([P, HALF], F32, name="acc", tag="bank%d" % (2 * s + h))
-                product(acc[:], w1_code, w1_scale, t, x_code[h][:], x_scale[:, half(h)])
-                nc.scalar.copy(y_s[:, half(h)], acc[:])
+                product(acc[:], w1_code[t], w1_scale[t], 0, x_code[:, half(h)], x_scale[:, half(h)])
+                copies[0 if (s, h) == (0, 1) else 1](y_s[:, half(h)], acc[:])
             y.append(y_s)
 
         for h in range(2):
-            cols = slice(h * N // 2, (h + 1) * N // 2)
             nc.scalar.copy(
-                w2_bf[:].rearrange("p (n j) -> p n j", j=PACK)[:, cols].rearrange("p (c i) j -> p c j i", i=4),
-                w2_raw[:, :, cols].rearrange("p j (c i) -> p c j i", i=4),
+                w2_bf[h][:].rearrange("p (c i) j -> p c j i", i=4),
+                w2_raw[:, :, half(h)].rearrange("p j (c i) -> p c j i", i=4),
             )
 
         a = [keep.tile([P, V], F32, name="a%d" % s) for s in range(PACK)]
@@ -133,27 +141,38 @@ def tile_picked_sortpair_none_p_kernel(tc, x_words, x_scales, w1, w2, offs, la, 
                 fetch(a, s + 2, la_t)
             else:
                 h = s + 2 - PACK
-                quantize(w2_code, w2_scale, w2_bf, h * N // 2, (h + 1) * N // 2)
+                quantize(w2_code[h], w2_scale[h], w2_bf[h][:].rearrange("p n j -> p (n j)"))
             nc.vector.tensor_copy(z[:].indirect(lb_t[:]), high[s][:])
             if s + 1 < PACK:
-                nc.scalar.copy(z_bf[:, :, t], z[:])
-            else:
-                for h in range(2):
-                    lo, mid, hi = h * HALF, h * HALF + TAIL_SPLIT, (h + 1) * HALF
-                    nc.vector.tensor_copy(z_bf[:, lo:mid, t], z[:, lo:mid])
-                    nc.scalar.copy(z_bf[:, mid:hi, t], z[:, mid:hi])
+                for c, (lo, hi) in enumerate(CHUNKS):
+                    nc.scalar.copy(z_bf[c][:, :, t], z[:, lo:hi])
 
-        z_flat = z_bf[:].rearrange("p j t -> p (j t)")
-        for h in range(2):
-            quantize(z_code, z_scale, z_flat, h * HALF, (h + 1) * HALF)
+        def round_last_plane(c):
+            lo, hi = CHUNKS[c]
+            split = (hi - lo) * 11 // 16
+            nc.vector.tensor_copy(z_bf[c][:, :split, t], z[:, lo : lo + split])
+            nc.scalar.copy(z_bf[c][:, split:, t], z[:, lo + split : hi])
 
+        round_last_plane(0)
+        for c in range(len(CHUNKS)):
+            if c + 1 < len(CHUNKS):
+                round_last_plane(c + 1)
+            quantize(z_code[c], z_scale[c], z_bf[c][:].rearrange("p j t -> p (j t)"))
+
+        out_pairs = out.rearrange("(g b p) j -> g p b j", b=2, p=P)
+        for c in range(2):
+            lo, hi = CHUNKS[c]
+            for g in range(2):
+                acc = psum.tile([P, 2, hi - lo], F32, name="acc", tag="bank%d" % (2 * c + g))
+                for block in range(2):
+                    product(acc[:, block, :], w2_code[g], w2_scale[g], block, z_code[c][:], z_scale[c][:])
+                res = keep.tile([P, 2, hi - lo], F32, name="res_narrow%d_%d" % (c, g))
+                copies[1 - g](res[:], acc[:])
+                nc.sync.dma_start(out_pairs[g][:, :, lo:hi], res[:])
+        lo, hi = CHUNKS[2]
         for m in range(N // P):
-            res = keep.tile([P, S], F32, name="res%d" % m)
-            for h in range(2):
-                acc = psum.tile([P, HALF], F32, name="acc", tag="bank%d" % (2 * m + h))
-                product(acc[:], w2_code, w2_scale, m, z_code[:, half(h)], z_scale[:, half(h)])
-                if h == 0:
-                    nc.scalar.copy(res[:, half(h)], acc[:])
-                else:
-                    nc.vector.tensor_copy(res[:, half(h)], acc[:])
-            nc.sync.dma_start(out[m * P : (m + 1) * P, :], res[:])
+            acc = psum.tile([P, hi - lo], F32, name="acc", tag="bank%d" % (4 + m))
+            product(acc[:], w2_code[m // 2], w2_scale[m // 2], m % 2, z_code[2][:], z_scale[2][:])
+            res = keep.tile([P, hi - lo], F32, name="res_wide%d" % m)
+            copies[1 - m % 2](res[:], acc[:])
+            nc.sync.dma_start(out[m * P : (m + 1) * P, lo:hi], res[:])

from contextlib import ExitStack

import concourse.mybir as mybir

K, T, S, V, H, N = 512, 2048, 512, 256, 512, 512
FLOPS = 2 * K * H * S + 2 * H * N * S

F32 = mybir.dt.float32
BF16 = mybir.dt.bfloat16
I32 = mybir.dt.int32
U32 = mybir.dt.uint32
U16 = mybir.dt.uint16
U8 = mybir.dt.uint8
FP8X4 = mybir.dt.float8_e4m3fn_x4
ALU = mybir.AluOpType

P = 128
PACK = 4
HALF = S // 2
PLANE_ORDER = (0, 2, 3, 1)
CHUNKS = ((0, 128), (128, 256), (256, 512))


def tile_picked_sortpair_none_p_kernel(tc, x_words, x_scales, w1, w2, offs, la, lb, out):
    nc = tc.nc
    with ExitStack() as ctx:
        keep = ctx.enter_context(tc.tile_pool(name="keep", bufs=1))
        ring = ctx.enter_context(tc.tile_pool(name="ring", bufs=3))
        psum = ctx.enter_context(tc.psum_pool(name="psum", bufs=1))

        def tiles(name, count, shape, dtype):
            return [keep.tile(shape, dtype, name="%s%d" % (name, i), align_bytes=64) for i in range(count)]

        def half(h):
            return slice(h * HALF, (h + 1) * HALF)

        offs_t = keep.tile([P, S // 16], U16, name="offs_t")
        la_t = keep.tile([P, V // 16], U16, name="la_t")
        lb_t = keep.tile([P, V // 16], U16, name="lb_t")
        words_all = keep.tile([P, T], U32, name="words_all", align_bytes=64)
        scales_all = keep.tile([P, T], U8, name="scales_all", align_bytes=64)
        scales_picked = keep.tile([P, S], U8, name="scales_picked", align_bytes=64)
        x_scale = keep.tile([P, S], U8, name="x_scale", align_bytes=64)
        x_code = keep.tile([P, S], U32, name="x_code", align_bytes=64)
        w1_head = keep.tile([P, 2, H], F32, name="w1_head", align_bytes=64)
        w1_last = keep.tile([P, 2, H], F32, name="w1_last", align_bytes=64)
        w1_bf = [
            keep.tile([P, 2, P, PACK], BF16, name="w1_bf0", align_bytes=64),
            keep.tile([P, 2, P, PACK], BF16, name="w1_bf1", tag="late", align_bytes=64),
        ]
        w1_code = tiles("w1_code", PACK, [P, P], U32)
        w1_scale = tiles("w1_scale", PACK, [P, P], U8)
        w2_bf = tiles("w2_bf", 2, [P, HALF, PACK], BF16)
        w2_code = tiles("w2_code", 2, [P, HALF], U32)
        w2_scale = tiles("w2_scale", 2, [P, HALF], U8)
        z_bf = [keep.tile([P, hi - lo, PACK], BF16, name="z_bf%d" % lo, align_bytes=64) for lo, hi in CHUNKS]
        z_code = [keep.tile([P, hi - lo], U32, name="z_code%d" % lo, align_bytes=64) for lo, hi in CHUNKS]
        z_scale = [keep.tile([P, hi - lo], U8, name="z_scale%d" % lo, align_bytes=64) for lo, hi in CHUNKS]

        nc.vector.memset(scales_all[:].bitcast(I32), 0)
        nc.vector.memset(x_scale[:].bitcast(I32), 0)

        w1_rows = w1.rearrange("(p j) c -> p j c", j=PACK)
        words_hbm = x_words[0].rearrange("p n t -> p (n t)").bitcast(I32)
        nc.sync.dma_start(offs_t[:], offs)
        nc.sync.dma_start(words_all[:, : T // 2].bitcast(I32), words_hbm[:, : T // 2])
        nc.sync.dma_start(scales_all[0:P:8, :].bitcast(I32), x_scales[0].bitcast(I32))
        nc.sync.dma_start(words_all[:, T // 2 :].bitcast(I32), words_hbm[:, T // 2 :])
        nc.sync.dma_start(w1_head[:], w1_rows[:, :2])
        nc.sync.dma_start(w1_last[:], w1_rows[:, 2:])
        nc.sync.dma_start(la_t[:], la)
        nc.sync.dma_start(lb_t[:], lb)

        nc.vector.tensor_copy(scales_picked[:], scales_all[:].indirect(offs_t[:]))
        for c in range(4):
            nc.scalar.dma_start(x_scale[c:P:32, :].bitcast(I32), scales_picked[8 * c : P : 32, :].bitcast(I32))
        nc.vector.tensor_copy(x_code[:], words_all[:].indirect(offs_t[:]))

        def quantize(code, scale, src):
            nc.vector.quantize_mx(out=code[:].bitcast(FP8X4), scales=scale[:], in_=src)

        def product(acc, w_code, w_scale, block, rhs, rhs_scale):
            cols = slice(block * P, (block + 1) * P)
            nc.tensor.matmul_mx(
                out=acc,
                lhsT=w_code[:, cols].bitcast(FP8X4),
                lhsT_scale=w_scale[:, cols],
                rhs=rhs.bitcast(FP8X4),
                rhs_scale=rhs_scale,
                start=True,
                stop=True,
            )

        head_src = w1_head[:].rearrange("p j (m u v) -> p v m u j", u=2, v=2)
        last_src = w1_last[:].rearrange("p j (m u v) -> p v m u j", u=2, v=2)
        copies = (nc.vector.tensor_copy, nc.scalar.copy)
        for v in range(2):
            copies[v](w1_bf[v][:, :, :, :2].rearrange("p u m j -> p m u j"), head_src[:, v])
        for u in range(2):
            nc.vector.tensor_copy(w1_bf[0][:, u, :, 2:], last_src[:, 0, :, u])
        nc.scalar.copy(w1_bf[1][:, :, :, 2:].rearrange("p u m j -> p m u j"), last_src[:, 1])
        for t in PLANE_ORDER:
            quantize(w1_code[t], w1_scale[t], w1_bf[t % 2][:, t // 2].rearrange("p m j -> p (m j)"))
        w2_raw = keep.tile([P, PACK, N], F32, name="w2_raw", tag="late", align_bytes=64)
        nc.sync.dma_start(w2_raw[:], w2.rearrange("(p j) c -> p j c", j=PACK))

        y = []
        for s, t in enumerate(PLANE_ORDER):
            y_s = keep.tile([P, S], F32, name="y%d" % s)
            for h in range(2):
                acc = psum.tile([P, HALF], F32, name="acc", tag="bank%d" % (2 * s + h))
                product(acc[:], w1_code[t], w1_scale[t], 0, x_code[:, half(h)], x_scale[:, half(h)])
                copies[0 if (s, h) == (0, 1) else 1](y_s[:, half(h)], acc[:])
            y.append(y_s)

        for h in range(2):
            nc.scalar.copy(
                w2_bf[h][:].rearrange("p (c i) j -> p c j i", i=4),
                w2_raw[:, :, half(h)].rearrange("p j (c i) -> p c j i", i=4),
            )

        a = [keep.tile([P, V], F32, name="a%d" % s) for s in range(PACK)]
        b = [keep.tile([P, V], F32, name="b%d" % s) for s in range(PACK)]
        low = [keep.tile([P, V], F32, name="low%d" % s) for s in range(PACK)]
        high = [keep.tile([P, V], F32, name="high%d" % s) for s in range(PACK)]

        def fetch(dst, s, lst):
            nc.vector.tensor_copy(dst[s][:], y[s][:].indirect(lst[:]))

        fetch(a, 0, la_t)
        fetch(b, 0, lb_t)
        fetch(a, 1, la_t)
        for s, t in enumerate(PLANE_ORDER):
            nc.vector.tensor_tensor(low[s][:], a[s][:], b[s][:], ALU.min)
            nc.vector.tensor_tensor(high[s][:], a[s][:], b[s][:], ALU.max)
            if s + 1 < PACK:
                fetch(b, s + 1, lb_t)
            z = ring.tile([P, S], F32, name="z")
            nc.vector.tensor_copy(z[:].indirect(la_t[:]), low[s][:])
            if s + 2 < PACK:
                fetch(a, s + 2, la_t)
            else:
                h = s + 2 - PACK
                quantize(w2_code[h], w2_scale[h], w2_bf[h][:].rearrange("p n j -> p (n j)"))
            nc.vector.tensor_copy(z[:].indirect(lb_t[:]), high[s][:])
            if s + 1 < PACK:
                for c, (lo, hi) in enumerate(CHUNKS):
                    nc.scalar.copy(z_bf[c][:, :, t], z[:, lo:hi])

        def round_last_plane(c):
            lo, hi = CHUNKS[c]
            split = (hi - lo) * 11 // 16
            nc.vector.tensor_copy(z_bf[c][:, :split, t], z[:, lo : lo + split])
            nc.scalar.copy(z_bf[c][:, split:, t], z[:, lo + split : hi])

        round_last_plane(0)
        for c in range(len(CHUNKS)):
            if c + 1 < len(CHUNKS):
                round_last_plane(c + 1)
            quantize(z_code[c], z_scale[c], z_bf[c][:].rearrange("p j t -> p (j t)"))

        out_pairs = out.rearrange("(g b p) j -> g p b j", b=2, p=P)
        for c in range(2):
            lo, hi = CHUNKS[c]
            for g in range(2):
                acc = psum.tile([P, 2, hi - lo], F32, name="acc", tag="bank%d" % (2 * c + g))
                for block in range(2):
                    product(acc[:, block, :], w2_code[g], w2_scale[g], block, z_code[c][:], z_scale[c][:])
                res = keep.tile([P, 2, hi - lo], F32, name="res_narrow%d_%d" % (c, g))
                copies[1 - g](res[:], acc[:])
                nc.sync.dma_start(out_pairs[g][:, :, lo:hi], res[:])
        lo, hi = CHUNKS[2]
        for m in range(N // P):
            acc = psum.tile([P, hi - lo], F32, name="acc", tag="bank%d" % (4 + m))
            product(acc[:], w2_code[m // 2], w2_scale[m // 2], m % 2, z_code[2][:], z_scale[2][:])
            res = keep.tile([P, hi - lo], F32, name="res_wide%d" % m)
            copies[1 - m % 2](res[:], acc[:])
            nc.sync.dma_start(out[m * P : (m + 1) * P, lo:hi], res[:])
